import numpy as np
import ml_dtypes


def mxq(x, axis, fmt="e4m3"):
    dtype, down = {"e4m3": (ml_dtypes.float8_e4m3fn, 7), "e5m2": (ml_dtypes.float8_e5m2, 14)}[fmt]
    v = np.moveaxis(np.asarray(x, np.float32).astype(ml_dtypes.bfloat16).astype(np.float64), axis, -1)
    blocks = v.reshape(v.shape[:-1] + (-1, 32))
    amax = np.abs(blocks).max(-1, keepdims=True)
    byte = np.maximum(np.where(amax > 0, np.frexp(amax)[1] - 1 + 127, 0) - down, 1)
    scale = np.exp2(byte - 127.0)
    codes = (blocks / scale).astype(np.float32).astype(dtype).astype(np.float64)
    return np.moveaxis((codes * scale).reshape(v.shape), -1, axis)


WIDE = False


def mx_kscale(k, group=512):
    if not WIDE:
        return np.ones(k)
    levels = np.array([10, -10, 5, -5, 0])
    if group != 512:
        return np.exp2(np.random.permutation(np.resize(levels, k // group))).repeat(group)
    if k % 512:
        return np.exp2(np.random.permutation(np.resize(levels, k // 32))).repeat(32)
    a = np.empty((k // 512, 16))
    for p in range(k // 512):
        a[p, :8] = np.random.permutation(np.resize(levels, 8))
        for g in range(8):
            far = levels[np.abs(levels - a[p, g]) >= 10]
            a[p, g + 8] = far[np.random.randint(len(far))]
    return np.exp2(a.ravel()).repeat(32)


def f64(x):
    return np.asarray(x).astype(np.float64)


def gelu(v):
    return 0.5 * v * (1.0 + np.tanh(0.7978845608028654 * (v + 0.044715 * v ** 3)))


K, R, M, N = 1024, 256, 512, 512


def setup_inputs():
    n = np.random.standard_normal
    s = mx_kscale(K)[:, None]
    z = mx_kscale(R, 0)
    return {
        "x": (n((K, N)) * s).astype(np.float32),
        "w": (n((K, M)) / np.sqrt(K) / s).astype(np.float32),
        "a": (n((K, R)) / np.sqrt(K) / s * z).astype(np.float32),
        "bb": (n((R, M)) / np.sqrt(R) / z[:, None]).astype(np.float32),
        "b": (0.5 * n((M, 1))).astype(np.float32),
    }


def reference(x, w, a, bb, b):
    xq = mxq(f64(x), 0, "e4m3")
    z = mxq(f64(a), 0, "e4m3").T @ xq
    y = (mxq(f64(w), 0, "e4m3").T @ xq) + (mxq(f64(bb), 0, "e4m3").T @ mxq(z, 0, "e4m3"))
    y = y + f64(b)
    y = gelu(y)
    return y

@@ -1,0 +1,182 @@
+from contextlib import ExitStack
+
+import concourse.mybir as mybir
+
+K, R, M, N = 1024, 256, 512, 512
+FLOPS = 2 * N * (K * R + K * M + R * M)
+
+F32 = mybir.dt.float32
+BF16 = mybir.dt.bfloat16
+U32 = mybir.dt.uint32
+U8 = mybir.dt.uint8
+FP8X4 = mybir.dt.float8_e4m3fn_x4
+ACT = mybir.ActivationFunctionType
+ALU = mybir.AluOpType
+
+P = 128
+PACK = 4
+K_PASS = P * PACK
+PASSES = K // K_PASS
+HALF = 256
+RT = 64
+
+
+def tile_rows_lora_gelu_bias_kernel(tc, x, w, a, bb, b, out):
+    nc = tc.nc
+    with ExitStack() as ctx:
+        sb = ctx.enter_context(tc.tile_pool(name="sb", bufs=1))
+        ps = ctx.enter_context(tc.psum_pool(name="ps", bufs=1))
+        ctx.enter_context(tc.manual_schedule())
+
+        def tile(name, shape, dtype):
+            return sb.tile(shape, dtype, name=name, align_bytes=64)
+
+        def rows(src, g, c0, width):
+            return src[g * K_PASS : (g + 1) * K_PASS, c0 : c0 + width].rearrange("(p j) c -> p j c", j=PACK)
+
+        a_raw = [tile("a_raw%d" % g, [P, PACK, R], F32) for g in range(PASSES)]
+        x_raw = [tile("x_raw%d" % g, [P, PACK, N], F32) for g in range(PASSES)]
+        w_raw = [[tile("w_raw%d%d" % (h, g), [P, PACK, HALF], F32) for g in range(PASSES)] for h in range(2)]
+        bb_raw = tile("bb_raw", [P, PACK, HALF], F32)
+        bias_rows = tile("bias_rows", [P, P], F32)
+        bias_cols = tile("bias_cols", [P, P], F32)
+        warm = tile("warm", [P, 8], F32)
+
+        a_bf = [tile("a_bf%d" % g, [P, R, PACK], BF16) for g in range(PASSES)]
+        x_bf = [[tile("x_bf%d%d" % (g, h), [P, HALF, PACK], BF16) for h in range(2)] for g in range(PASSES)]
+        w_bf = [[tile("w_bf%d%d" % (h, g), [P, HALF, PACK], BF16) for g in range(PASSES)] for h in range(2)]
+        bb_bf = tile("bb_bf", [P, HALF, PACK], BF16)
+        z_rows = tile("z_rows", [P, PACK, N], BF16)
+        z_bf = [tile("z_bf%d" % h, [P, HALF, PACK], BF16) for h in range(2)]
+
+        def planes(name, width):
+            return tile(name + "_codes", [P, width], U32), tile(name + "_scales", [P, width], U8)
+
+        a_mx = [planes("a%d" % g, R + RT) for g in range(PASSES)]
+        x_mx = [planes("x%d" % g, N) for g in range(PASSES)]
+        w_mx = [[planes("w%d%d" % (h, g), HALF) for g in range(PASSES)] for h in range(2)]
+        bb_mx = planes("bb", HALF)
+        z_mx = planes("z", N)
+
+        whole = [ps.tile([P, N], F32, name="whole%d" % i) for i in range(4)]
+        rowb = [ps.tile([P, N], F32, name="rowb%d" % i) for i in range(4)]
+        part = [tile("part%d" % i, [P, N], F32) for i in range(4)]
+        pre = [tile("pre%d" % i, [P, N], F32) for i in range(4)]
+        res = [tile("res%d" % i, [P, N], F32) for i in range(4)]
+
+        def copy(eng, dst, src):
+            if eng == "v":
+                nc.vector.tensor_copy(out=dst, in_=src)
+            else:
+                nc.scalar.copy(out=dst, in_=src)
+
+        def interleave(eng, dst, src):
+            copy(eng, dst.rearrange("p (c i) t -> p c t i", i=4), src.rearrange("p t (c i) -> p c t i", i=4))
+
+        def deal_a(eng, g):
+            copy(eng, a_bf[g][:].rearrange("p (j m) t -> p m t j", j=PACK), a_raw[g][:].rearrange("p t (m j) -> p m t j", j=PACK))
+
+        def quant(mx, c0, src):
+            width = src.shape[1]
+            nc.vector.quantize_mx(out=mx[0][:, c0 : c0 + width].bitcast(FP8X4), scales=mx[1][:, c0 : c0 + width], in_=src.rearrange("p c t -> p (c t)"))
+
+        def mm(dst, lhs, c0, rhs, r0, r1, start, stop):
+            nc.tensor.matmul_mx(
+                out=dst[:],
+                lhsT=lhs[0][r0:r1, c0 : c0 + P].bitcast(FP8X4),
+                lhsT_scale=lhs[1][r0:r1, c0 : c0 + P],
+                rhs=rhs[0][r0:r1, :].bitcast(FP8X4),
+                rhs_scale=rhs[1][r0:r1, :],
+                start=start,
+                stop=stop,
+            )
+
+        def quant_a(g):
+            quant(a_mx[g], 0, a_bf[g][:])
+            quant(a_mx[g], R, a_bf[g][:, 0:RT, :])
+
+        def z_pass(g):
+            for j in range(PACK):
+                mm(whole[j], a_mx[g], RT * j, x_mx[g], 0, P, g == 0, g == PASSES - 1)
+
+        def w_mm(mt, g):
+            mm(whole[mt], w_mx[mt // 2][g], P * (mt % 2), x_mx[g], 0, P, g == 0, g == PASSES - 1)
+
+        def bb_mm(mt):
+            r0 = RT * (mt // 2)
+            mm(rowb[mt], bb_mx, P * (mt % 2), z_mx, r0, r0 + RT, True, True)
+
+        def finish(mt, bank):
+            nc.vector.tensor_tensor(out=pre[mt][:], in0=bank[:], in1=part[mt][:], op=ALU.add)
+            nc.scalar.activation(out=res[mt][:], in_=pre[mt][:], func=ACT.Gelu_apprx_tanh, bias=bias_cols[:, 32 * mt : 32 * mt + 1])
+            nc.sync.dma_start(out=out[P * mt : P * (mt + 1), :], in_=res[mt][:])
+
+        nc.sync.dma_start(out=a_raw[0][:], in_=rows(a, 0, 0, R))
+        nc.sync.dma_start(out=x_raw[0][:], in_=rows(x, 0, 0, N))
+        nc.sync.dma_start(out=x_raw[1][:], in_=rows(x, 1, 0, N))
+        nc.sync.dma_start(out=a_raw[1][:], in_=rows(a, 1, 0, R))
+        bb4 = bb.rearrange("(p j) c -> p j c", j=PACK)
+        nc.sync.dma_start(out=bb_raw[0:RT], in_=bb4[:, :, 0:HALF])
+        nc.sync.dma_start(out=bb_raw[RT:P, 0:3, :], in_=bb4[:, 1:4, HALF:M])
+        nc.sync.dma_start(out=bb_raw[RT:P, 3:4, :], in_=bb4[:, 0:1, HALF:M])
+        for h in range(2):
+            for g in range(PASSES):
+                nc.sync.dma_start(out=w_raw[h][g][:], in_=rows(w, g, HALF * h, HALF))
+
+        nc.vector.memset(bias_rows[:], 0.0)
+        nc.vector.memset(warm[:], 0.0)
+        nc.scalar.activation(out=warm[:, 0:1], in_=warm[:, 1:2], func=ACT.Gelu_apprx_tanh)
+        nc.scalar.dma_start(
+            out=bias_rows[0:P:32, :].rearrange("q (c k) -> q c k", k=32),
+            in_=b.rearrange("(c q k) o -> q c (k o)", q=4, k=32),
+        )
+
+        deal_a("v", 0)
+        quant_a(0)
+        nc.vector.transpose(out=bias_cols[:], in_=bias_rows[:])
+        for g in range(PASSES):
+            interleave("v", x_bf[g][0][:], x_raw[g][:, :, 0:HALF])
+            interleave("s", x_bf[g][1][:], x_raw[g][:, :, HALF:N])
+            quant(x_mx[g], 0, x_bf[g][0][:])
+            quant(x_mx[g], HALF, x_bf[g][1][:])
+            if g == 0:
+                z_pass(0)
+        deal_a("v", 1)
+        quant_a(1)
+        z_pass(1)
+        interleave("v", bb_bf[:], bb_raw[:])
+        copy("s", z_rows[:, 0, :], whole[0][:])
+        copy("v", z_rows[:, 1, :], whole[1][:])
+        copy("s", z_rows[:, 2, :], whole[2][:])
+        quant(bb_mx, 0, bb_bf[:])
+        copy("v", z_rows[:, 3, :], whole[3][:])
+        interleave("s", w_bf[0][0][:], w_raw[0][0][:])
+        interleave("v", z_bf[0][:], z_rows[:, :, 0:HALF])
+        interleave("v", z_bf[1][:], z_rows[:, :, HALF:N])
+        quant(z_mx, 0, z_bf[0][:])
+        quant(w_mx[0][0], 0, w_bf[0][0][:])
+        quant(z_mx, HALF, z_bf[1][:])
+        w_mm(0, 0)
+        w_mm(1, 0)
+        interleave("s", w_bf[0][1][:], w_raw[0][1][:])
+        for mt in (0, 2, 1, 3):
+            bb_mm(mt)
+        interleave("v", w_bf[1][0][:], w_raw[1][0][:])
+        quant(w_mx[0][1], 0, w_bf[0][1][:])
+        w_mm(0, 1)
+        w_mm(1, 1)
+        copy("s", part[0][:], rowb[0][:])
+        copy("s", part[1][:], rowb[1][:])
+        interleave("v", w_bf[1][1][:], w_raw[1][1][:])
+        quant(w_mx[1][0], 0, w_bf[1][0][:])
+        w_mm(2, 0)
+        w_mm(3, 0)
+        copy("s", part[2][:], rowb[2][:])
+        quant(w_mx[1][1], 0, w_bf[1][1][:])
+        w_mm(2, 1)
+        w_mm(3, 1)
+        finish(0, whole[0])
+        copy("s", part[3][:], rowb[3][:])
+        finish(1, whole[1])
+        finish(2, whole[2])
+        finish(3, whole[3])

@@ -42,7 +42,7 @@ def tile_rows_lora_gelu_bias_kernel(tc, x, w, a, bb, b, out):
         bias_cols = tile("bias_cols", [P, P], F32)
         warm = tile("warm", [P, 8], F32)
 
-        a_bf = [tile("a_bf%d" % g, [P, R, PACK], BF16) for g in range(PASSES)]
+        a_bf = [[tile("a_bf%d%d" % (g, u), [P, P, PACK], BF16) for u in range(2)] for g in range(PASSES)]
         x_bf = [[tile("x_bf%d%d" % (g, h), [P, HALF, PACK], BF16) for h in range(2)] for g in range(PASSES)]
         w_bf = [[tile("w_bf%d%d" % (h, g), [P, HALF, PACK], BF16) for g in range(PASSES)] for h in range(2)]
         bb_bf = tile("bb_bf", [P, HALF, PACK], BF16)
@@ -73,8 +73,9 @@ def tile_rows_lora_gelu_bias_kernel(tc, x, w, a, bb, b, out):
         def interleave(eng, dst, src):
             copy(eng, dst.rearrange("p (c i) t -> p c t i", i=4), src.rearrange("p t (c i) -> p c t i", i=4))
 
-        def deal_a(eng, g):
-            copy(eng, a_bf[g][:].rearrange("p (j m) t -> p m t j", j=PACK), a_raw[g][:].rearrange("p t (m j) -> p m t j", j=PACK))
+        def deal_a(eng, g, u):
+            src = a_raw[g][:].rearrange("p t (m j) -> p m t j", j=PACK)[:, :, :, 2 * u : 2 * u + 2]
+            copy(eng, a_bf[g][u][:].rearrange("p (j m) t -> p m t j", j=2), src)
 
         def quant(mx, c0, src):
             width = src.shape[1]
@@ -92,91 +93,103 @@ def tile_rows_lora_gelu_bias_kernel(tc, x, w, a, bb, b, out):
             )
 
         def quant_a(g):
-            quant(a_mx[g], 0, a_bf[g][:])
-            quant(a_mx[g], R, a_bf[g][:, 0:RT, :])
+            quant(a_mx[g], 0, a_bf[g][0][:])
+            quant(a_mx[g], P, a_bf[g][1][:])
+            quant(a_mx[g], R, a_bf[g][0][:, 0:RT, :])
 
         def z_pass(g):
             for j in range(PACK):
                 mm(whole[j], a_mx[g], RT * j, x_mx[g], 0, P, g == 0, g == PASSES - 1)
 
-        def w_mm(mt, g):
-            mm(whole[mt], w_mx[mt // 2][g], P * (mt % 2), x_mx[g], 0, P, g == 0, g == PASSES - 1)
+        def w_mm(mt, g, first):
+            mm(whole[mt], w_mx[mt // 2][g], P * (mt % 2), x_mx[g], 0, P, first, not first)
 
         def bb_mm(mt):
             r0 = RT * (mt // 2)
             mm(rowb[mt], bb_mx, P * (mt % 2), z_mx, r0, r0 + RT, True, True)
 
-        def finish(mt, bank):
+        def add(mt, bank):
             nc.vector.tensor_tensor(out=pre[mt][:], in0=bank[:], in1=part[mt][:], op=ALU.add)
+
+        def finish(mt):
             nc.scalar.activation(out=res[mt][:], in_=pre[mt][:], func=ACT.Gelu_apprx_tanh, bias=bias_cols[:, 32 * mt : 32 * mt + 1])
             nc.sync.dma_start(out=out[P * mt : P * (mt + 1), :], in_=res[mt][:])
 
-        nc.sync.dma_start(out=a_raw[0][:], in_=rows(a, 0, 0, R))
-        nc.sync.dma_start(out=x_raw[0][:], in_=rows(x, 0, 0, N))
-        nc.sync.dma_start(out=x_raw[1][:], in_=rows(x, 1, 0, N))
-        nc.sync.dma_start(out=a_raw[1][:], in_=rows(a, 1, 0, R))
-        bb4 = bb.rearrange("(p j) c -> p j c", j=PACK)
-        nc.sync.dma_start(out=bb_raw[0:RT], in_=bb4[:, :, 0:HALF])
-        nc.sync.dma_start(out=bb_raw[RT:P, 0:3, :], in_=bb4[:, 1:4, HALF:M])
-        nc.sync.dma_start(out=bb_raw[RT:P, 3:4, :], in_=bb4[:, 0:1, HALF:M])
-        for h in range(2):
-            for g in range(PASSES):
-                nc.sync.dma_start(out=w_raw[h][g][:], in_=rows(w, g, HALF * h, HALF))
-
         nc.vector.memset(bias_rows[:], 0.0)
         nc.vector.memset(warm[:], 0.0)
-        nc.scalar.activation(out=warm[:, 0:1], in_=warm[:, 1:2], func=ACT.Gelu_apprx_tanh)
         nc.scalar.dma_start(
             out=bias_rows[0:P:32, :].rearrange("q (c k) -> q c k", k=32),
             in_=b.rearrange("(c q k) o -> q c (k o)", q=4, k=32),
         )
+        nc.scalar.activation(out=warm[:, 0:1], in_=warm[:, 1:2], func=ACT.Gelu_apprx_tanh)
+        bb4 = bb.rearrange("(p j) c -> p j c", j=PACK)
+        nc.sync.dma_start(out=a_raw[0][:], in_=rows(a, 0, 0, R))
+        nc.sync.dma_start(out=x_raw[0][:], in_=rows(x, 0, 0, N))
+        nc.sync.dma_start(out=x_raw[1][:], in_=rows(x, 1, 0, N))
+        nc.sync.dma_start(out=a_raw[1][:], in_=rows(a, 1, 0, R))
+        nc.sync.dma_start(out=w_raw[0][0][:], in_=rows(w, 0, 0, HALF))
+        nc.sync.dma_start(out=w_raw[0][1][:], in_=rows(w, 1, 0, HALF))
+        nc.sync.dma_start(out=bb_raw[0:RT], in_=bb4[:, :, 0:HALF])
+        nc.sync.dma_start(out=bb_raw[RT:P, 0:3, :], in_=bb4[:, 1:4, HALF:M])
+        nc.sync.dma_start(out=bb_raw[RT:P, 3:4, :], in_=bb4[:, 0:1, HALF:M])
+        nc.sync.dma_start(out=w_raw[1][0][:], in_=rows(w, 0, HALF, HALF))
+        nc.sync.dma_start(out=w_raw[1][1][:], in_=rows(w, 1, HALF, HALF))
 
-        deal_a("v", 0)
+        deal_a("v", 0, 0)
+        deal_a("s", 0, 1)
         quant_a(0)
-        nc.vector.transpose(out=bias_cols[:], in_=bias_rows[:])
-        for g in range(PASSES):
-            interleave("v", x_bf[g][0][:], x_raw[g][:, :, 0:HALF])
-            interleave("s", x_bf[g][1][:], x_raw[g][:, :, HALF:N])
-            quant(x_mx[g], 0, x_bf[g][0][:])
-            quant(x_mx[g], HALF, x_bf[g][1][:])
-            if g == 0:
-                z_pass(0)
-        deal_a("v", 1)
+        interleave("v", x_bf[0][0][:], x_raw[0][:, :, 0:HALF])
+        interleave("s", x_bf[0][1][:], x_raw[0][:, :, HALF:N])
+        quant(x_mx[0], 0, x_bf[0][0][:])
+        quant(x_mx[0], HALF, x_bf[0][1][:])
+        z_pass(0)
+        interleave("v", x_bf[1][0][:], x_raw[1][:, :, 0:HALF])
+        interleave("s", x_bf[1][1][:], x_raw[1][:, :, HALF:N])
+        quant(x_mx[1], 0, x_bf[1][0][:])
+        deal_a("v", 1, 0)
+        deal_a("s", 1, 1)
+        quant(x_mx[1], HALF, x_bf[1][1][:])
         quant_a(1)
         z_pass(1)
-        interleave("v", bb_bf[:], bb_raw[:])
+
+        interleave("v", w_bf[0][0][:], w_raw[0][0][:])
         copy("s", z_rows[:, 0, :], whole[0][:])
-        copy("v", z_rows[:, 1, :], whole[1][:])
+        copy("s", z_rows[:, 1, :], whole[1][:])
+        nc.vector.transpose(out=bias_cols[:], in_=bias_rows[:])
+        quant(w_mx[0][0], 0, w_bf[0][0][:])
+        interleave("v", w_bf[0][1][:], w_raw[0][1][:])
         copy("s", z_rows[:, 2, :], whole[2][:])
-        quant(bb_mx, 0, bb_bf[:])
         copy("v", z_rows[:, 3, :], whole[3][:])
-        interleave("s", w_bf[0][0][:], w_raw[0][0][:])
+        w_mm(0, 0, True)
+        w_mm(1, 0, True)
+        interleave("s", bb_bf[:], bb_raw[:])
+        quant(w_mx[0][1], 0, w_bf[0][1][:])
+        w_mm(0, 1, False)
+        w_mm(1, 1, False)
         interleave("v", z_bf[0][:], z_rows[:, :, 0:HALF])
         interleave("v", z_bf[1][:], z_rows[:, :, HALF:N])
+        quant(bb_mx, 0, bb_bf[:])
         quant(z_mx, 0, z_bf[0][:])
-        quant(w_mx[0][0], 0, w_bf[0][0][:])
         quant(z_mx, HALF, z_bf[1][:])
-        w_mm(0, 0)
-        w_mm(1, 0)
-        interleave("s", w_bf[0][1][:], w_raw[0][1][:])
+        copy("s", part[0][:], whole[0][:])
+        copy("s", part[1][:], whole[1][:])
         for mt in (0, 2, 1, 3):
             bb_mm(mt)
-        interleave("v", w_bf[1][0][:], w_raw[1][0][:])
-        quant(w_mx[0][1], 0, w_bf[0][1][:])
-        w_mm(0, 1)
-        w_mm(1, 1)
-        copy("s", part[0][:], rowb[0][:])
-        copy("s", part[1][:], rowb[1][:])
+        interleave("s", w_bf[1][0][:], w_raw[1][0][:])
         interleave("v", w_bf[1][1][:], w_raw[1][1][:])
-        quant(w_mx[1][0], 0, w_bf[1][0][:])
-        w_mm(2, 0)
-        w_mm(3, 0)
-        copy("s", part[2][:], rowb[2][:])
+        add(0, rowb[0])
         quant(w_mx[1][1], 0, w_bf[1][1][:])
-        w_mm(2, 1)
-        w_mm(3, 1)
-        finish(0, whole[0])
+        w_mm(2, 1, True)
+        w_mm(3, 1, True)
+        quant(w_mx[1][0], 0, w_bf[1][0][:])
+        w_mm(2, 0, False)
+        w_mm(3, 0, False)
+        copy("s", part[2][:], rowb[2][:])
+        add(1, rowb[1])
         copy("s", part[3][:], rowb[3][:])
-        finish(1, whole[1])
-        finish(2, whole[2])
-        finish(3, whole[3])
+        finish(0)
+        add(2, whole[2])
+        finish(1)
+        add(3, whole[3])
+        finish(2)
+        finish(3)

@@ -10,186 +10,208 @@ BF16 = mybir.dt.bfloat16
 U32 = mybir.dt.uint32
 U8 = mybir.dt.uint8
 FP8X4 = mybir.dt.float8_e4m3fn_x4
-ACT = mybir.ActivationFunctionType
-ALU = mybir.AluOpType
 
 P = 128
 PACK = 4
 K_PASS = P * PACK
 PASSES = K // K_PASS
+M_TILES = M // P
+ROW_TILE = R // PACK
 HALF = 256
-RT = 64
+SQUARE = 32
+RUN = 4
 
 
 def tile_rows_lora_gelu_bias_kernel(tc, x, w, a, bb, b, out):
     nc = tc.nc
     with ExitStack() as ctx:
-        sb = ctx.enter_context(tc.tile_pool(name="sb", bufs=1))
-        ps = ctx.enter_context(tc.psum_pool(name="ps", bufs=1))
+        sbuf = ctx.enter_context(tc.tile_pool(name="sbuf", bufs=1))
+        psum = ctx.enter_context(tc.psum_pool(name="psum", bufs=1))
         ctx.enter_context(tc.manual_schedule())
 
         def tile(name, shape, dtype):
-            return sb.tile(shape, dtype, name=name, align_bytes=64)
+            return sbuf.tile(shape, dtype, name=name, align_bytes=64)
 
-        def rows(src, g, c0, width):
-            return src[g * K_PASS : (g + 1) * K_PASS, c0 : c0 + width].rearrange("(p j) c -> p j c", j=PACK)
+        def mx_operand(name, width):
+            return tile(name + "_codes", [P, width], U32), tile(name + "_scales", [P, width], U8)
 
         a_raw = [tile("a_raw%d" % g, [P, PACK, R], F32) for g in range(PASSES)]
         x_raw = [tile("x_raw%d" % g, [P, PACK, N], F32) for g in range(PASSES)]
-        w_raw = [[tile("w_raw%d%d" % (h, g), [P, PACK, HALF], F32) for g in range(PASSES)] for h in range(2)]
+        w_raw = [tile("w_raw%d" % g, [P, PACK, M], F32) for g in range(PASSES)]
         bb_raw = tile("bb_raw", [P, PACK, HALF], F32)
         bias_rows = tile("bias_rows", [P, P], F32)
         bias_cols = tile("bias_cols", [P, P], F32)
-        warm = tile("warm", [P, 8], F32)
+        table_probe = tile("table_probe", [P, 8], F32)
 
-        a_bf = [[tile("a_bf%d%d" % (g, u), [P, P, PACK], BF16) for u in range(2)] for g in range(PASSES)]
+        a_bf = [[tile("a_bf%d%d" % (g, u), [P, 2 * ROW_TILE, PACK], BF16) for u in range(2)] for g in range(PASSES)]
         x_bf = [[tile("x_bf%d%d" % (g, h), [P, HALF, PACK], BF16) for h in range(2)] for g in range(PASSES)]
-        w_bf = [[tile("w_bf%d%d" % (h, g), [P, HALF, PACK], BF16) for g in range(PASSES)] for h in range(2)]
+        w0_bf = [tile("w0_bf%d" % h, [P, HALF, PACK], BF16) for h in range(2)]
+        w1_bf = [tile("w1_bf%d" % mt, [P, P, PACK], BF16) for mt in range(M_TILES)]
         bb_bf = tile("bb_bf", [P, HALF, PACK], BF16)
         z_rows = tile("z_rows", [P, PACK, N], BF16)
         z_bf = [tile("z_bf%d" % h, [P, HALF, PACK], BF16) for h in range(2)]
 
-        def planes(name, width):
-            return tile(name + "_codes", [P, width], U32), tile(name + "_scales", [P, width], U8)
+        a_mx = [mx_operand("a%d" % g, R + ROW_TILE) for g in range(PASSES)]
+        x_mx = [mx_operand("x%d" % g, N) for g in range(PASSES)]
+        w_mx = [mx_operand("w%d" % g, M) for g in range(PASSES)]
+        bb_mx = mx_operand("bb", HALF)
+        z_mx = mx_operand("z", N)
 
-        a_mx = [planes("a%d" % g, R + RT) for g in range(PASSES)]
-        x_mx = [planes("x%d" % g, N) for g in range(PASSES)]
-        w_mx = [[planes("w%d%d" % (h, g), HALF) for g in range(PASSES)] for h in range(2)]
-        bb_mx = planes("bb", HALF)
-        z_mx = planes("z", N)
+        whole_bank = [psum.tile([P, N], F32, name="whole_bank%d" % i) for i in range(M_TILES)]
+        branch_bank = [psum.tile([P, N], F32, name="branch_bank%d" % mt) for mt in range(M_TILES)]
+        branch = [tile("branch%d" % mt, [P, N], F32) for mt in range(M_TILES)]
+        y_sum = [tile("y_sum%d" % mt, [P, N], F32) for mt in range(M_TILES)]
+        result = [tile("result%d" % mt, [P, N], F32) for mt in range(M_TILES)]
 
-        whole = [ps.tile([P, N], F32, name="whole%d" % i) for i in range(4)]
-        rowb = [ps.tile([P, N], F32, name="rowb%d" % i) for i in range(4)]
-        part = [tile("part%d" % i, [P, N], F32) for i in range(4)]
-        pre = [tile("pre%d" % i, [P, N], F32) for i in range(4)]
-        res = [tile("res%d" % i, [P, N], F32) for i in range(4)]
+        vector_copy = nc.vector.tensor_copy
+        scalar_copy = nc.scalar.copy
 
-        def copy(eng, dst, src):
-            if eng == "v":
-                nc.vector.tensor_copy(out=dst, in_=src)
-            else:
-                nc.scalar.copy(out=dst, in_=src)
+        def load_pass(dst, src, g):
+            rows = src[g * K_PASS : (g + 1) * K_PASS, :]
+            nc.sync.dma_start(out=dst[:], in_=rows.rearrange("(p t) c -> p t c", t=PACK))
 
-        def interleave(eng, dst, src):
-            copy(eng, dst.rearrange("p (c i) t -> p c t i", i=4), src.rearrange("p t (c i) -> p c t i", i=4))
+        def interleave(copy, dst, src):
+            copy(out=dst.rearrange("p (c i) t -> p c t i", i=RUN), in_=src.rearrange("p t (c i) -> p c t i", i=RUN))
 
-        def deal_a(eng, g, u):
+        def deal_a(copy, g, u):
             src = a_raw[g][:].rearrange("p t (m j) -> p m t j", j=PACK)[:, :, :, 2 * u : 2 * u + 2]
-            copy(eng, a_bf[g][u][:].rearrange("p (j m) t -> p m t j", j=2), src)
+            copy(out=a_bf[g][u][:].rearrange("p (j m) t -> p m t j", j=2), in_=src)
 
-        def quant(mx, c0, src):
-            width = src.shape[1]
-            nc.vector.quantize_mx(out=mx[0][:, c0 : c0 + width].bitcast(FP8X4), scales=mx[1][:, c0 : c0 + width], in_=src.rearrange("p c t -> p (c t)"))
+        def quantize(operand, first_column, src):
+            codes, scales = operand
+            columns = slice(first_column, first_column + src.shape[1])
+            nc.vector.quantize_mx(
+                out=codes[:, columns].bitcast(FP8X4),
+                scales=scales[:, columns],
+                in_=src.rearrange("p c t -> p (c t)"),
+            )
 
-        def mm(dst, lhs, c0, rhs, r0, r1, start, stop):
+        def quantize_a(g):
+            quantize(a_mx[g], 0, a_bf[g][0][:])
+            quantize(a_mx[g], 2 * ROW_TILE, a_bf[g][1][:])
+            quantize(a_mx[g], R, a_bf[g][0][:, 0:ROW_TILE, :])
+
+        def matmul(bank, stationary, first_column, moving, partitions, start, stop):
+            columns = slice(first_column, first_column + P)
             nc.tensor.matmul_mx(
-                out=dst[:],
-                lhsT=lhs[0][r0:r1, c0 : c0 + P].bitcast(FP8X4),
-                lhsT_scale=lhs[1][r0:r1, c0 : c0 + P],
-                rhs=rhs[0][r0:r1, :].bitcast(FP8X4),
-                rhs_scale=rhs[1][r0:r1, :],
+                out=bank[:],
+                lhsT=stationary[0][partitions, columns].bitcast(FP8X4),
+                lhsT_scale=stationary[1][partitions, columns],
+                rhs=moving[0][partitions, :].bitcast(FP8X4),
+                rhs_scale=moving[1][partitions, :],
                 start=start,
                 stop=stop,
             )
 
-        def quant_a(g):
-            quant(a_mx[g], 0, a_bf[g][0][:])
-            quant(a_mx[g], P, a_bf[g][1][:])
-            quant(a_mx[g], R, a_bf[g][0][:, 0:RT, :])
-
-        def z_pass(g):
+        def z_matmuls(g):
             for j in range(PACK):
-                mm(whole[j], a_mx[g], RT * j, x_mx[g], 0, P, g == 0, g == PASSES - 1)
+                matmul(whole_bank[j], a_mx[g], ROW_TILE * j, x_mx[g], slice(0, P), g == 0, g == PASSES - 1)
 
-        def w_mm(mt, g, first):
-            mm(whole[mt], w_mx[mt // 2][g], P * (mt % 2), x_mx[g], 0, P, first, not first)
+        def w_matmul(mt, g):
+            matmul(whole_bank[mt], w_mx[g], P * mt, x_mx[g], slice(0, P), g == 0, g == PASSES - 1)
 
-        def bb_mm(mt):
-            r0 = RT * (mt // 2)
-            mm(rowb[mt], bb_mx, P * (mt % 2), z_mx, r0, r0 + RT, True, True)
+        def bb_matmul(mt):
+            half, tile_in_half = divmod(mt, 2)
+            partitions = slice(ROW_TILE * half, ROW_TILE * (half + 1))
+            matmul(branch_bank[mt], bb_mx, P * tile_in_half, z_mx, partitions, True, True)
 
-        def add(mt, bank):
-            nc.vector.tensor_tensor(out=pre[mt][:], in0=bank[:], in1=part[mt][:], op=ALU.add)
+        def interleave_w1(mt):
+            interleave(vector_copy, w1_bf[mt][:], w_raw[1][:, :, P * mt : P * (mt + 1)])
 
-        def finish(mt):
-            nc.scalar.activation(out=res[mt][:], in_=pre[mt][:], func=ACT.Gelu_apprx_tanh, bias=bias_cols[:, 32 * mt : 32 * mt + 1])
-            nc.sync.dma_start(out=out[P * mt : P * (mt + 1), :], in_=res[mt][:])
+        def quantize_w1(mt):
+            quantize(w_mx[1], P * mt, w1_bf[mt][:])
+
+        def copy_branch(mt):
+            scalar_copy(out=branch[mt][:], in_=branch_bank[mt][:])
+
+        def add_sums(mt):
+            nc.vector.tensor_tensor(out=y_sum[mt][:], in0=whole_bank[mt][:], in1=branch[mt][:], op=mybir.AluOpType.add)
+
+        def gelu_and_store(mt):
+            nc.scalar.activation(
+                out=result[mt][:],
+                in_=y_sum[mt][:],
+                func=mybir.ActivationFunctionType.Gelu_apprx_tanh,
+                bias=bias_cols[:, SQUARE * mt : SQUARE * mt + 1],
+            )
+            nc.sync.dma_start(out=out[P * mt : P * (mt + 1), :], in_=result[mt][:])
 
         nc.vector.memset(bias_rows[:], 0.0)
-        nc.vector.memset(warm[:], 0.0)
+        nc.vector.memset(table_probe[:], 0.0)
         nc.scalar.dma_start(
-            out=bias_rows[0:P:32, :].rearrange("q (c k) -> q c k", k=32),
-            in_=b.rearrange("(c q k) o -> q c (k o)", q=4, k=32),
+            out=bias_rows[0:P:SQUARE, :].rearrange("q (mt i) -> q mt i", i=SQUARE),
+            in_=b.rearrange("(mt q i) o -> q mt (i o)", q=P // SQUARE, i=SQUARE),
         )
-        nc.scalar.activation(out=warm[:, 0:1], in_=warm[:, 1:2], func=ACT.Gelu_apprx_tanh)
-        bb4 = bb.rearrange("(p j) c -> p j c", j=PACK)
-        nc.sync.dma_start(out=a_raw[0][:], in_=rows(a, 0, 0, R))
-        nc.sync.dma_start(out=x_raw[0][:], in_=rows(x, 0, 0, N))
-        nc.sync.dma_start(out=x_raw[1][:], in_=rows(x, 1, 0, N))
-        nc.sync.dma_start(out=a_raw[1][:], in_=rows(a, 1, 0, R))
-        nc.sync.dma_start(out=w_raw[0][0][:], in_=rows(w, 0, 0, HALF))
-        nc.sync.dma_start(out=w_raw[0][1][:], in_=rows(w, 1, 0, HALF))
-        nc.sync.dma_start(out=bb_raw[0:RT], in_=bb4[:, :, 0:HALF])
-        nc.sync.dma_start(out=bb_raw[RT:P, 0:3, :], in_=bb4[:, 1:4, HALF:M])
-        nc.sync.dma_start(out=bb_raw[RT:P, 3:4, :], in_=bb4[:, 0:1, HALF:M])
-        nc.sync.dma_start(out=w_raw[1][0][:], in_=rows(w, 0, HALF, HALF))
-        nc.sync.dma_start(out=w_raw[1][1][:], in_=rows(w, 1, HALF, HALF))
+        nc.scalar.activation(out=table_probe[:, 0:1], in_=table_probe[:, 1:2], func=mybir.ActivationFunctionType.Gelu_apprx_tanh)
 
-        deal_a("v", 0, 0)
-        deal_a("s", 0, 1)
-        quant_a(0)
-        interleave("v", x_bf[0][0][:], x_raw[0][:, :, 0:HALF])
-        interleave("s", x_bf[0][1][:], x_raw[0][:, :, HALF:N])
-        quant(x_mx[0], 0, x_bf[0][0][:])
-        quant(x_mx[0], HALF, x_bf[0][1][:])
-        z_pass(0)
-        interleave("v", x_bf[1][0][:], x_raw[1][:, :, 0:HALF])
-        interleave("s", x_bf[1][1][:], x_raw[1][:, :, HALF:N])
-        quant(x_mx[1], 0, x_bf[1][0][:])
-        deal_a("v", 1, 0)
-        deal_a("s", 1, 1)
-        quant(x_mx[1], HALF, x_bf[1][1][:])
-        quant_a(1)
-        z_pass(1)
+        load_pass(a_raw[0], a, 0)
+        load_pass(x_raw[0], x, 0)
+        load_pass(x_raw[1], x, 1)
+        load_pass(a_raw[1], a, 1)
+        load_pass(w_raw[0], w, 0)
+        bb_rows = bb.rearrange("(p t) c -> p t c", t=PACK)
+        nc.sync.dma_start(out=bb_raw[0:ROW_TILE], in_=bb_rows[:, :, 0:HALF])
+        nc.sync.dma_start(out=bb_raw[ROW_TILE:P, 0 : PACK - 1, :], in_=bb_rows[:, 1:PACK, HALF:M])
+        nc.sync.dma_start(out=bb_raw[ROW_TILE:P, PACK - 1 : PACK, :], in_=bb_rows[:, 0:1, HALF:M])
+        load_pass(w_raw[1], w, 1)
 
-        interleave("v", w_bf[0][0][:], w_raw[0][0][:])
-        copy("s", z_rows[:, 0, :], whole[0][:])
-        copy("s", z_rows[:, 1, :], whole[1][:])
+        deal_a(vector_copy, 0, 0)
+        deal_a(scalar_copy, 0, 1)
+        quantize_a(0)
+        interleave(vector_copy, x_bf[0][0][:], x_raw[0][:, :, 0:HALF])
+        interleave(scalar_copy, x_bf[0][1][:], x_raw[0][:, :, HALF:N])
+        quantize(x_mx[0], 0, x_bf[0][0][:])
+        quantize(x_mx[0], HALF, x_bf[0][1][:])
+        z_matmuls(0)
+
+        interleave(vector_copy, x_bf[1][0][:], x_raw[1][:, :, 0:HALF])
+        interleave(scalar_copy, x_bf[1][1][:], x_raw[1][:, :, HALF:N])
+        quantize(x_mx[1], 0, x_bf[1][0][:])
+        deal_a(vector_copy, 1, 0)
+        deal_a(scalar_copy, 1, 1)
+        quantize(x_mx[1], HALF, x_bf[1][1][:])
+        quantize_a(1)
+        z_matmuls(1)
+
+        scalar_copy(out=z_rows[:, 0, :], in_=whole_bank[0][:])
+        vector_copy(out=z_rows[:, 1, :], in_=whole_bank[1][:])
+        scalar_copy(out=z_rows[:, 2, :], in_=whole_bank[2][:])
+        interleave(vector_copy, w0_bf[0][:], w_raw[0][:, :, 0:HALF])
+        scalar_copy(out=z_rows[:, 3, :], in_=whole_bank[3][:])
         nc.vector.transpose(out=bias_cols[:], in_=bias_rows[:])
-        quant(w_mx[0][0], 0, w_bf[0][0][:])
-        interleave("v", w_bf[0][1][:], w_raw[0][1][:])
-        copy("s", z_rows[:, 2, :], whole[2][:])
-        copy("v", z_rows[:, 3, :], whole[3][:])
-        w_mm(0, 0, True)
-        w_mm(1, 0, True)
-        interleave("s", bb_bf[:], bb_raw[:])
-        quant(w_mx[0][1], 0, w_bf[0][1][:])
-        w_mm(0, 1, False)
-        w_mm(1, 1, False)
-        interleave("v", z_bf[0][:], z_rows[:, :, 0:HALF])
-        interleave("v", z_bf[1][:], z_rows[:, :, HALF:N])
-        quant(bb_mx, 0, bb_bf[:])
-        quant(z_mx, 0, z_bf[0][:])
-        quant(z_mx, HALF, z_bf[1][:])
-        copy("s", part[0][:], whole[0][:])
-        copy("s", part[1][:], whole[1][:])
-        for mt in (0, 2, 1, 3):
-            bb_mm(mt)
-        interleave("s", w_bf[1][0][:], w_raw[1][0][:])
-        interleave("v", w_bf[1][1][:], w_raw[1][1][:])
-        add(0, rowb[0])
-        quant(w_mx[1][1], 0, w_bf[1][1][:])
-        w_mm(2, 1, True)
-        w_mm(3, 1, True)
-        quant(w_mx[1][0], 0, w_bf[1][0][:])
-        w_mm(2, 0, False)
-        w_mm(3, 0, False)
-        copy("s", part[2][:], rowb[2][:])
-        add(1, rowb[1])
-        copy("s", part[3][:], rowb[3][:])
-        finish(0)
-        add(2, whole[2])
-        finish(1)
-        add(3, whole[3])
-        finish(2)
-        finish(3)
+        quantize(w_mx[0], 0, w0_bf[0][:])
+        w_matmul(0, 0)
+        w_matmul(1, 0)
+
+        interleave(vector_copy, z_bf[0][:], z_rows[:, :, 0:HALF])
+        interleave(scalar_copy, z_bf[1][:], z_rows[:, :, HALF:N])
+        interleave(vector_copy, bb_bf[:], bb_raw[:])
+        quantize(z_mx, 0, z_bf[0][:])
+        quantize(z_mx, HALF, z_bf[1][:])
+        quantize(bb_mx, 0, bb_bf[:])
+        for tile_in_half in range(2):
+            for half in range(2):
+                bb_matmul(2 * half + tile_in_half)
+
+        interleave(scalar_copy, w0_bf[1][:], w_raw[0][:, :, HALF:M])
+        quantize(w_mx[0], HALF, w0_bf[1][:])
+        interleave_w1(0)
+        interleave_w1(1)
+        quantize_w1(0)
+        quantize_w1(1)
+        w_matmul(0, 1)
+        w_matmul(1, 1)
+        w_matmul(2, 0)
+        w_matmul(3, 0)
+        interleave_w1(2)
+        interleave_w1(3)
+        quantize_w1(2)
+        quantize_w1(3)
+        w_matmul(2, 1)
+        w_matmul(3, 1)
+
+        for mt in range(M_TILES):
+            copy_branch(mt)
+        for mt in range(M_TILES):
+            add_sums(mt)
+            gelu_and_store(mt)

from contextlib import ExitStack

import concourse.mybir as mybir

K, R, M, N = 1024, 256, 512, 512
FLOPS = 2 * N * (K * R + K * M + R * M)

F32 = mybir.dt.float32
BF16 = mybir.dt.bfloat16
U32 = mybir.dt.uint32
U8 = mybir.dt.uint8
FP8X4 = mybir.dt.float8_e4m3fn_x4

P = 128
PACK = 4
K_PASS = P * PACK
PASSES = K // K_PASS
M_TILES = M // P
ROW_TILE = R // PACK
HALF = 256
SQUARE = 32
RUN = 4


def tile_rows_lora_gelu_bias_kernel(tc, x, w, a, bb, b, out):
    nc = tc.nc
    with ExitStack() as ctx:
        sbuf = ctx.enter_context(tc.tile_pool(name="sbuf", bufs=1))
        psum = ctx.enter_context(tc.psum_pool(name="psum", bufs=1))
        ctx.enter_context(tc.manual_schedule())

        def tile(name, shape, dtype):
            return sbuf.tile(shape, dtype, name=name, align_bytes=64)

        def mx_operand(name, width):
            return tile(name + "_codes", [P, width], U32), tile(name + "_scales", [P, width], U8)

        a_raw = [tile("a_raw%d" % g, [P, PACK, R], F32) for g in range(PASSES)]
        x_raw = [tile("x_raw%d" % g, [P, PACK, N], F32) for g in range(PASSES)]
        w_raw = [tile("w_raw%d" % g, [P, PACK, M], F32) for g in range(PASSES)]
        bb_raw = tile("bb_raw", [P, PACK, HALF], F32)
        bias_rows = tile("bias_rows", [P, P], F32)
        bias_cols = tile("bias_cols", [P, P], F32)
        table_probe = tile("table_probe", [P, 8], F32)

        a_bf = [[tile("a_bf%d%d" % (g, u), [P, 2 * ROW_TILE, PACK], BF16) for u in range(2)] for g in range(PASSES)]
        x_bf = [[tile("x_bf%d%d" % (g, h), [P, HALF, PACK], BF16) for h in range(2)] for g in range(PASSES)]
        w0_bf = [tile("w0_bf%d" % h, [P, HALF, PACK], BF16) for h in range(2)]
        w1_bf = [tile("w1_bf%d" % mt, [P, P, PACK], BF16) for mt in range(M_TILES)]
        bb_bf = tile("bb_bf", [P, HALF, PACK], BF16)
        z_rows = tile("z_rows", [P, PACK, N], BF16)
        z_bf = [tile("z_bf%d" % h, [P, HALF, PACK], BF16) for h in range(2)]

        a_mx = [mx_operand("a%d" % g, R + ROW_TILE) for g in range(PASSES)]
        x_mx = [mx_operand("x%d" % g, N) for g in range(PASSES)]
        w_mx = [mx_operand("w%d" % g, M) for g in range(PASSES)]
        bb_mx = mx_operand("bb", HALF)
        z_mx = mx_operand("z", N)

        whole_bank = [psum.tile([P, N], F32, name="whole_bank%d" % i) for i in range(M_TILES)]
        branch_bank = [psum.tile([P, N], F32, name="branch_bank%d" % mt) for mt in range(M_TILES)]
        branch = [tile("branch%d" % mt, [P, N], F32) for mt in range(M_TILES)]
        y_sum = [tile("y_sum%d" % mt, [P, N], F32) for mt in range(M_TILES)]
        result = [tile("result%d" % mt, [P, N], F32) for mt in range(M_TILES)]

        vector_copy = nc.vector.tensor_copy
        scalar_copy = nc.scalar.copy

        def load_pass(dst, src, g):
            rows = src[g * K_PASS : (g + 1) * K_PASS, :]
            nc.sync.dma_start(out=dst[:], in_=rows.rearrange("(p t) c -> p t c", t=PACK))

        def interleave(copy, dst, src):
            copy(out=dst.rearrange("p (c i) t -> p c t i", i=RUN), in_=src.rearrange("p t (c i) -> p c t i", i=RUN))

        def deal_a(copy, g, u):
            src = a_raw[g][:].rearrange("p t (m j) -> p m t j", j=PACK)[:, :, :, 2 * u : 2 * u + 2]
            copy(out=a_bf[g][u][:].rearrange("p (j m) t -> p m t j", j=2), in_=src)

        def quantize(operand, first_column, src):
            codes, scales = operand
            columns = slice(first_column, first_column + src.shape[1])
            nc.vector.quantize_mx(
                out=codes[:, columns].bitcast(FP8X4),
                scales=scales[:, columns],
                in_=src.rearrange("p c t -> p (c t)"),
            )

        def quantize_a(g):
            quantize(a_mx[g], 0, a_bf[g][0][:])
            quantize(a_mx[g], 2 * ROW_TILE, a_bf[g][1][:])
            quantize(a_mx[g], R, a_bf[g][0][:, 0:ROW_TILE, :])

        def matmul(bank, stationary, first_column, moving, partitions, start, stop):
            columns = slice(first_column, first_column + P)
            nc.tensor.matmul_mx(
                out=bank[:],
                lhsT=stationary[0][partitions, columns].bitcast(FP8X4),
                lhsT_scale=stationary[1][partitions, columns],
                rhs=moving[0][partitions, :].bitcast(FP8X4),
                rhs_scale=moving[1][partitions, :],
                start=start,
                stop=stop,
            )

        def z_matmuls(g):
            for j in range(PACK):
                matmul(whole_bank[j], a_mx[g], ROW_TILE * j, x_mx[g], slice(0, P), g == 0, g == PASSES - 1)

        def w_matmul(mt, g):
            matmul(whole_bank[mt], w_mx[g], P * mt, x_mx[g], slice(0, P), g == 0, g == PASSES - 1)

        def bb_matmul(mt):
            half, tile_in_half = divmod(mt, 2)
            partitions = slice(ROW_TILE * half, ROW_TILE * (half + 1))
            matmul(branch_bank[mt], bb_mx, P * tile_in_half, z_mx, partitions, True, True)

        def interleave_w1(mt):
            interleave(vector_copy, w1_bf[mt][:], w_raw[1][:, :, P * mt : P * (mt + 1)])

        def quantize_w1(mt):
            quantize(w_mx[1], P * mt, w1_bf[mt][:])

        def copy_branch(mt):
            scalar_copy(out=branch[mt][:], in_=branch_bank[mt][:])

        def add_sums(mt):
            nc.vector.tensor_tensor(out=y_sum[mt][:], in0=whole_bank[mt][:], in1=branch[mt][:], op=mybir.AluOpType.add)

        def gelu_and_store(mt):
            nc.scalar.activation(
                out=result[mt][:],
                in_=y_sum[mt][:],
                func=mybir.ActivationFunctionType.Gelu_apprx_tanh,
                bias=bias_cols[:, SQUARE * mt : SQUARE * mt + 1],
            )
            nc.sync.dma_start(out=out[P * mt : P * (mt + 1), :], in_=result[mt][:])

        nc.vector.memset(bias_rows[:], 0.0)
        nc.vector.memset(table_probe[:], 0.0)
        nc.scalar.dma_start(
            out=bias_rows[0:P:SQUARE, :].rearrange("q (mt i) -> q mt i", i=SQUARE),
            in_=b.rearrange("(mt q i) o -> q mt (i o)", q=P // SQUARE, i=SQUARE),
        )
        nc.scalar.activation(out=table_probe[:, 0:1], in_=table_probe[:, 1:2], func=mybir.ActivationFunctionType.Gelu_apprx_tanh)

        load_pass(a_raw[0], a, 0)
        load_pass(x_raw[0], x, 0)
        load_pass(x_raw[1], x, 1)
        load_pass(a_raw[1], a, 1)
        load_pass(w_raw[0], w, 0)
        bb_rows = bb.rearrange("(p t) c -> p t c", t=PACK)
        nc.sync.dma_start(out=bb_raw[0:ROW_TILE], in_=bb_rows[:, :, 0:HALF])
        nc.sync.dma_start(out=bb_raw[ROW_TILE:P, 0 : PACK - 1, :], in_=bb_rows[:, 1:PACK, HALF:M])
        nc.sync.dma_start(out=bb_raw[ROW_TILE:P, PACK - 1 : PACK, :], in_=bb_rows[:, 0:1, HALF:M])
        load_pass(w_raw[1], w, 1)

        deal_a(vector_copy, 0, 0)
        deal_a(scalar_copy, 0, 1)
        quantize_a(0)
        interleave(vector_copy, x_bf[0][0][:], x_raw[0][:, :, 0:HALF])
        interleave(scalar_copy, x_bf[0][1][:], x_raw[0][:, :, HALF:N])
        quantize(x_mx[0], 0, x_bf[0][0][:])
        quantize(x_mx[0], HALF, x_bf[0][1][:])
        z_matmuls(0)

        interleave(vector_copy, x_bf[1][0][:], x_raw[1][:, :, 0:HALF])
        interleave(scalar_copy, x_bf[1][1][:], x_raw[1][:, :, HALF:N])
        quantize(x_mx[1], 0, x_bf[1][0][:])
        deal_a(vector_copy, 1, 0)
        deal_a(scalar_copy, 1, 1)
        quantize(x_mx[1], HALF, x_bf[1][1][:])
        quantize_a(1)
        z_matmuls(1)

        scalar_copy(out=z_rows[:, 0, :], in_=whole_bank[0][:])
        vector_copy(out=z_rows[:, 1, :], in_=whole_bank[1][:])
        scalar_copy(out=z_rows[:, 2, :], in_=whole_bank[2][:])
        interleave(vector_copy, w0_bf[0][:], w_raw[0][:, :, 0:HALF])
        scalar_copy(out=z_rows[:, 3, :], in_=whole_bank[3][:])
        nc.vector.transpose(out=bias_cols[:], in_=bias_rows[:])
        quantize(w_mx[0], 0, w0_bf[0][:])
        w_matmul(0, 0)
        w_matmul(1, 0)

        interleave(vector_copy, z_bf[0][:], z_rows[:, :, 0:HALF])
        interleave(scalar_copy, z_bf[1][:], z_rows[:, :, HALF:N])
        interleave(vector_copy, bb_bf[:], bb_raw[:])
        quantize(z_mx, 0, z_bf[0][:])
        quantize(z_mx, HALF, z_bf[1][:])
        quantize(bb_mx, 0, bb_bf[:])
        for tile_in_half in range(2):
            for half in range(2):
                bb_matmul(2 * half + tile_in_half)

        interleave(scalar_copy, w0_bf[1][:], w_raw[0][:, :, HALF:M])
        quantize(w_mx[0], HALF, w0_bf[1][:])
        interleave_w1(0)
        interleave_w1(1)
        quantize_w1(0)
        quantize_w1(1)
        w_matmul(0, 1)
        w_matmul(1, 1)
        w_matmul(2, 0)
        w_matmul(3, 0)
        interleave_w1(2)
        interleave_w1(3)
        quantize_w1(2)
        quantize_w1(3)
        w_matmul(2, 1)
        w_matmul(3, 1)

        for mt in range(M_TILES):
            copy_branch(mt)
        for mt in range(M_TILES):
            add_sums(mt)
            gelu_and_store(mt)
